import numpy as np
import ml_dtypes


def mxq(x, axis, fmt="e4m3"):
    dtype, down = {"e4m3": (ml_dtypes.float8_e4m3fn, 7), "e5m2": (ml_dtypes.float8_e5m2, 14)}[fmt]
    v = np.moveaxis(np.asarray(x, np.float32).astype(ml_dtypes.bfloat16).astype(np.float64), axis, -1)
    blocks = v.reshape(v.shape[:-1] + (-1, 32))
    amax = np.abs(blocks).max(-1, keepdims=True)
    byte = np.maximum(np.where(amax > 0, np.frexp(amax)[1] - 1 + 127, 0) - down, 1)
    scale = np.exp2(byte - 127.0)
    codes = (blocks / scale).astype(np.float32).astype(dtype).astype(np.float64)
    return np.moveaxis((codes * scale).reshape(v.shape), -1, axis)


WIDE = False


def mx_kscale(k):
    if not WIDE:
        return np.ones(k)
    levels = np.array([10, -10, 5, -5, 0])
    if k % 512:
        return np.exp2(np.random.permutation(np.resize(levels, k // 32))).repeat(32)
    a = np.empty((k // 512, 16))
    for p in range(k // 512):
        a[p, :8] = np.random.permutation(np.resize(levels, 8))
        for g in range(8):
            far = levels[np.abs(levels - a[p, g]) >= 10]
            a[p, g + 8] = far[np.random.randint(len(far))]
    return np.exp2(a.ravel()).repeat(32)


def f64(x):
    return np.asarray(x).astype(np.float64)


def striped(idx):
    return np.tile(idx.reshape(-1, 16).T, (8, 1)).astype(np.uint16)


def unstriped(offs):
    return offs[:16].T.reshape(-1).astype(np.int64)


def striped8(idx):
    return np.concatenate([x.reshape(-1, 16).T for x in idx]).astype(np.uint16)


def runs(offs, k):
    lists = np.stack([offs[16 * r : 16 * r + 16].T.reshape(-1) for r in range(8)]).astype(np.int64)
    return lists[np.arange(k) % 512 // 64]


def pack_weight(w):
    k, n = w.shape
    w = f64(np.asarray(w, np.float32).astype(ml_dtypes.bfloat16)).reshape(k // 32, 32, n)
    amax = np.abs(w).max(1)
    byte = np.clip(np.where(amax > 0, np.frexp(amax)[1] - 1 + 127 - 7, 1), 1, 254)
    scaled = (w * np.exp2(127.0 - byte)[:, None, :]).reshape(k, n).astype(np.float32)
    words = np.ascontiguousarray(scaled.reshape(k // 512, 128, 4, n).transpose(0, 1, 3, 2)).astype(ml_dtypes.float8_e4m3fn).view(np.uint8)
    return words, np.ascontiguousarray(byte.astype(np.uint8).reshape(k // 512, 16, n))


def unpack_weight(words, scales):
    g, p, n, _ = words.shape
    vals = np.ascontiguousarray(words).view(ml_dtypes.float8_e4m3fn).astype(np.float64) * np.repeat(np.exp2(scales.astype(np.float64) - 127.0), 8, axis=1)[..., None]
    return vals.transpose(0, 1, 3, 2).reshape(g * 512, n)

def planes(y):
    n, m = y.shape
    v = y.astype(np.float32).astype(ml_dtypes.bfloat16).astype(np.float64).reshape(n // 32, 32, m)
    top = np.abs(v).max(1)
    byte = np.clip(np.where(top > 0, np.frexp(top)[1] - 1 + 127 - 7, 1), 1, 254)
    codes = (v * np.exp2(127.0 - byte)[:, None, :]).reshape(n, m).astype(np.float32).astype(ml_dtypes.float8_e4m3fn).view(np.uint8)
    words = codes.reshape(n // 512, 128, 4, m).transpose(0, 1, 3, 2)
    return np.ascontiguousarray(words), np.ascontiguousarray(byte.astype(np.uint8).reshape(n // 512, 16, m))


K, T, S, H, G = 512, 2048, 512, 512, 2048


def setup_inputs():
    n = np.random.standard_normal
    s = mx_kscale(K)[:, None]
    packed_xT = pack_weight(n((K, T)) * s)
    packed_w1 = pack_weight(n((K, H)) / np.sqrt(K) / s)
    packed_w2 = pack_weight(n((K, H)) / np.sqrt(K) / s)
    packed_dT = pack_weight(n((K, G)) / s)
    return {
        "x_words": packed_xT[0],
        "x_scales": packed_xT[1],
        "w1_words": packed_w1[0],
        "w1_scales": packed_w1[1],
        "w2_words": packed_w2[0],
        "w2_scales": packed_w2[1],
        "gs": (np.random.uniform(0.5, 1.5, (K, 1)) * s).astype(np.float32),
        "d_words": packed_dT[0],
        "d_scales": packed_dT[1],
        "offs": striped(np.random.permutation(T)[:S]),
        "two": striped(np.random.permutation(T)[:S]),
        "nb": striped8(np.stack([np.random.permutation(S) for _ in range(8)])),
        "kq": striped8(np.random.randint(0, G, (8, H))),
    }


def reference(x_words, x_scales, w1_words, w1_scales, w2_words, w2_scales, gs, d_words, d_scales, offs, two, nb, kq):
    d_kq = unpack_weight(d_words, d_scales)[np.arange(K)[:, None], runs(kq, K)]
    x_two = unpack_weight(x_words, x_scales)[:, unstriped(two)]
    c = unpack_weight(w2_words, w2_scales).T @ x_two
    xq = unpack_weight(x_words, x_scales)[:, unstriped(offs)]
    y = unpack_weight(w1_words, w1_scales).T @ xq
    vn = c - (np.tanh(y - (y[np.arange(H)[:, None], runs(nb, H)])))
    xn = y + 0.5 * vn
    z = f64(gs) * (vn - (np.tanh(xn - (xn[np.arange(H)[:, None], runs(nb, H)]))))
    out_0 = 0.0625 * ((d_kq.T @ mxq(z, 0, "e4m3")))
    return (out_0,) + planes(out_0)

@@ -1,0 +1,299 @@
+from contextlib import ExitStack
+
+import concourse.mybir as mybir
+
+F32 = mybir.dt.float32
+BF16 = mybir.dt.bfloat16
+I32 = mybir.dt.int32
+U32 = mybir.dt.uint32
+U16 = mybir.dt.uint16
+U8 = mybir.dt.uint8
+FP8X4 = mybir.dt.float8_e4m3fn_x4
+ACT = mybir.ActivationFunctionType
+ALU = mybir.AluOpType
+
+P = 128
+PACK = 4
+K, T, S, H = 512, 2048, 512, 512
+FLOPS = 3 * 2 * K * H * S
+HALF = 256
+CH = 128
+
+
+def words_of(ap):
+    return ap[0].rearrange("p n t -> p (n t)").bitcast(I32)
+
+
+def deal_words(eng, dst, src):
+    eng.tensor_copy(
+        out=dst[:].bitcast(I32).rearrange("p (t c i) -> p c t i", t=PACK, i=4),
+        in_=src[:].bitcast(I32).rearrange("p (c i t) -> p c t i", t=PACK, i=4),
+    )
+
+
+def deal_scales(eng, dst, src):
+    eng.tensor_copy(
+        out=dst[:].rearrange("p (t c i) -> p c t i", t=PACK, i=16),
+        in_=src[:].rearrange("p (c i t) -> p c t i", t=PACK, i=16),
+    )
+
+
+def tile_picked_symplec_none_po_kernel(
+    tc, x_words, x_scales, w1_words, w1_scales, w2_words, w2_scales, gs, d_words, d_scales,
+    offs, two, nb, kq, out_0, out_1, out_2,
+):
+    nc = tc.nc
+    with ExitStack() as ctx:
+        keep = ctx.enter_context(tc.tile_pool(name="keep", bufs=1))
+        psum = ctx.enter_context(tc.psum_pool(name="psum", bufs=1))
+
+        def sb(name, shape, dtype, tag=None):
+            return keep.tile(shape, dtype, name=name, tag=tag or name, align_bytes=64)
+
+        offs_t = keep.tile([P, S // 16], U16, name="offs_t")
+        two_t = keep.tile([P, S // 16], U16, name="two_t")
+        nb_t = keep.tile([P, S // 16], U16, name="nb_t")
+        kq_t = keep.tile([P, H // 16], U16, name="kq_t")
+        xw = sb("xw", [P, T], U32)
+        xs = sb("xs", [P, T], U8)
+        dw = sb("dw", [P, T], U32)
+        ds = sb("ds", [P, T], U8)
+        w1w = sb("w1w", [P, H], U32)
+        w2w = sb("w2w", [P, H], U32)
+        w1s = sb("w1s", [P, H], U8)
+        w2s = sb("w2s", [P, H], U8)
+        dsf = sb("dsf", [P, H], U8)
+        gs_t = sb("gs_t", [P, PACK], F32)
+        warm = sb("warm", [P, 8], F32)
+
+        nc.vector.memset(xs[:].bitcast(I32), 0)
+        nc.gpsimd.memset(warm[:], 0.0)
+        for tl in (w1s, w2s, ds, dsf):
+            nc.vector.memset(tl[:].bitcast(I32), 0)
+
+        def load_scales(tl, src, eng):
+            for q in range(4):
+                eng.dma_start(tl[32 * q : 32 * q + 4, :].bitcast(I32), src[0, 4 * q : 4 * q + 4, :].bitcast(I32))
+
+        nc.sync.dma_start(offs_t[:], offs)
+        nc.scalar.dma_start(w1w[:].bitcast(I32), words_of(w1_words))
+        nc.scalar.dma_start(gs_t[:], gs.rearrange("(p t) o -> p (t o)", t=PACK))
+        nc.scalar.dma_start(xw[:].bitcast(I32), words_of(x_words))
+        nc.scalar.activation(warm[:, 4:5], warm[:, 0:1], ACT.Tanh)
+        load_scales(xs, x_scales, nc.sync)
+        load_scales(w1s, w1_scales, nc.sync)
+        nc.sync.dma_start(two_t[:], two)
+        nc.sync.dma_start(nb_t[:], nb)
+        nc.sync.dma_start(w2w[:].bitcast(I32), words_of(w2_words))
+        nc.sync.dma_start(kq_t[:], kq)
+        for e in range(2):
+            nc.sync.dma_start(ds[e:P:16, :].bitcast(I32), d_scales[0, e:16:2, :].bitcast(I32))
+        load_scales(w2s, w2_scales, nc.gpsimd)
+        nc.sync.dma_start(dw[:].bitcast(I32), words_of(d_words))
+
+        xqs = sb("xqs", [P, S], U8)
+        x2s = sb("x2s", [P, S], U8)
+        xq = sb("xq", [P, S], U32)
+        x2 = sb("x2", [P, S], U32)
+        w1d = sb("w1d", [P, H], U32)
+        w2d = sb("w2d", [P, H], U32)
+        w1sd = sb("w1sd", [P, H], U8)
+        dd = sb("dd", [P, H], U32)
+        dsg = sb("dsg", [P, H], U8)
+        dsd = sb("dsd", [P, H], U8)
+
+        nc.vector.tensor_copy(xqs[:], xs[:].indirect(offs_t[:]))
+        deal_words(nc.vector, w1d, w1w)
+        deal_scales(nc.vector, w1sd, w1s)
+        nc.vector.tensor_copy(xq[:], xw[:].indirect(offs_t[:]))
+
+        def product(acc, lw, ls, rw, rs, t, cols):
+            m = slice(t * P, (t + 1) * P)
+            nc.tensor.matmul_mx(out=acc, lhsT=lw[:, m].bitcast(FP8X4), lhsT_scale=ls[:, m],
+                                rhs=rw[:, cols].bitcast(FP8X4), rhs_scale=rs[:, cols], start=True, stop=True)
+
+        full = slice(0, S)
+        y_ps = [psum.tile([P, S], F32, name="y_ps%d" % t, tag="a%d" % t) for t in range(PACK)]
+        c_ps = [psum.tile([P, S], F32, name="c_ps%d" % t, tag="b%d" % t) for t in range(PACK)]
+        for t in range(PACK):
+            product(y_ps[t][:], w1d, w1sd, xq, xqs, t, full)
+        nc.vector.tensor_copy(x2s[:], xs[:].indirect(two_t[:]))
+        nc.vector.tensor_copy(x2[:], xw[:].indirect(two_t[:]))
+        w2sd = sb("w2sd", [P, H], U8, tag="w1s")
+        deal_words(nc.vector, w2d, w2w)
+        deal_scales(nc.vector, w2sd, w2s)
+        for t in range(PACK):
+            product(c_ps[t][:], w2d, w2sd, x2, x2s, t, full)
+        nc.vector.tensor_copy(dsg[:], ds[:].indirect(kq_t[:]))
+        deal_scales(nc.vector, dsd, dsg)
+        for r, src in enumerate((0, 1, 16, 17)):
+            nc.sync.dma_start(dsf[r:P:32, :].bitcast(I32), dsd[src:P:32, :].bitcast(I32))
+
+        def diff(dst, win, cp, lo, n):
+            nc.vector.tensor_tensor(dst, win[:].indirect(nb_t[:, lo // 16 : (lo + n) // 16]), cp[:, lo : lo + n], ALU.subtract)
+
+        y_win = [sb("y_win%d" % t, [P, S], F32) for t in range(PACK)]
+        y_cp = [sb("y_cp%d" % t, [P, S], F32) for t in range(PACK)]
+        g1 = [sb("g1_%d" % t, [P, S], F32) for t in range(PACK)]
+        t1 = [sb("t1_%d" % t, [P, S], F32) for t in range(PACK)]
+        vn = [sb("vn_%d" % t, [P, S], F32) for t in range(PACK)]
+        gvn = [sb("gvn_%d" % t, [P, S], F32) for t in range(PACK)]
+        x_win = [sb("x_win%d" % t, [P, S], F32) for t in range(PACK)]
+        x_cp = [sb("x_cp%d" % t, [P, S], F32) for t in range(PACK)]
+
+        def pa(t):
+            nc.scalar.copy(y_win[t][:], y_ps[t][:])
+
+        def pb(t):
+            nc.scalar.copy(y_cp[t][:], y_ps[t][:])
+
+        def p1(t):
+            for lo in range(0, S, HALF):
+                diff(g1[t][:, lo : lo + HALF], y_win[t], y_cp[t], lo, HALF)
+
+        def pt(t):
+            nc.scalar.activation(t1[t][:], g1[t][:], ACT.Tanh)
+
+        def p2(t):
+            nc.vector.tensor_tensor(vn[t][:], t1[t][:], c_ps[t][:], ALU.add)
+
+        def p3(t):
+            nc.vector.scalar_tensor_tensor(x_win[t][:], vn[t][:], 0.5, y_cp[t][:], ALU.mult, ALU.add)
+
+        def p4(t):
+            nc.scalar.copy(x_cp[t][:], x_win[t][:])
+
+        def p5(t):
+            nc.scalar.activation(gvn[t][:], vn[t][:], ACT.Copy, scale=gs_t[:, t : t + 1])
+
+        pa(0)
+        pb(0)
+        p1(0)
+        pa(1)
+        pb(1)
+        p1(1)
+        pa(2)
+        pt(0)
+        pb(2)
+        p2(0)
+        p1(2)
+        p3(0)
+        pt(1)
+        pa(3)
+        pb(3)
+        p2(1)
+        p1(3)
+        p3(1)
+        pt(2)
+        p4(0)
+        p5(0)
+        pt(3)
+        p2(2)
+        p2(3)
+        p3(2)
+        p3(3)
+        p4(1)
+        p5(1)
+        p4(2)
+        p5(2)
+        p4(3)
+        p5(3)
+        dg = sb("dg", [P, H], U32, tag="t1_3")
+        nc.vector.tensor_copy(dg[:], dw[:].indirect(kq_t[:]))
+        deal_words(nc.vector, dd, dg)
+
+        out_rows = out_0.rearrange("(p t) n -> p t n", t=PACK)
+        o_codes = sb("o_codes", [P, S], U32)
+        o_scales = sb("o_scales", [P, S], U8)
+        n_ch = S // CH
+        g2, t2 = {}, {}
+        zp = [sb("zp_%d" % h, [P, PACK, CH], BF16) for h in range(n_ch)]
+        zi = [sb("zi_%d" % h, [P, CH, PACK], BF16) for h in range(n_ch)]
+        zc = [sb("zc_%d" % h, [P, CH], U32) for h in range(n_ch)]
+        zs = [sb("zs_%d" % h, [P, CH], U8) for h in range(n_ch)]
+        of = [sb("of_%d" % h, [P, PACK, CH], F32) for h in range(n_ch)]
+        oi = [sb("oi_%d" % h, [P, CH, PACK], BF16) for h in range(n_ch)]
+
+        o_ps = {}
+
+        def ga(h):
+            g2[h] = sb("g2_%d" % h, [P, PACK, CH], F32, tag=("g1_3", "g1_2", "t2_0", "t2_1")[h])
+            for t in range(PACK):
+                diff(g2[h][:, t, :], x_win[t], x_cp[t], h * CH, CH)
+
+        def th(h):
+            t2[h] = sb("t2_%d" % h, [P, PACK, CH], F32)
+            if h in ():
+                for t in range(PACK):
+                    nc.scalar.activation(t2[h][:, t, :], g2[h][:, t, :], ACT.Tanh)
+            else:
+                nc.scalar.activation(t2[h][:], g2[h][:], ACT.Tanh)
+
+        def zz(h):
+            for t in range(PACK):
+                nc.vector.scalar_tensor_tensor(zp[h][:, t, :], t2[h][:, t, :], gs_t[:, t : t + 1],
+                                               gvn[t][:, h * CH : (h + 1) * CH], ALU.mult, ALU.add)
+
+        def zw(h):
+            dst = zi[h][:].rearrange("p (c i) t -> p c t i", i=4)
+            src = zp[h][:].rearrange("p t (c i) -> p c t i", i=4)
+            if h in (3,):
+                nc.vector.tensor_copy(dst, src)
+            else:
+                nc.scalar.copy(dst, src)
+
+        def zq(h):
+            nc.vector.quantize_mx(out=zc[h][:].bitcast(FP8X4), scales=zs[h][:], in_=zi[h][:].rearrange("p n t -> p (n t)"))
+            o_ps[h] = psum.tile([P, PACK, CH], F32, name="o_ps%d" % h, tag="a%d" % h)
+            for t in range(PACK):
+                product(o_ps[h][:, t, :], dd, dsf, zc[h], zs[h], t, slice(0, CH))
+
+        def ow(h):
+            nc.scalar.activation(oi[h][:], o_ps[h][:].rearrange("p t n -> p n t"), ACT.Copy, scale=0.0625)
+
+        def oe(h):
+            nc.scalar.activation(of[h][:], o_ps[h][:], ACT.Copy, scale=0.0625)
+            nc.sync.dma_start(out_rows[:, :, h * CH : (h + 1) * CH], of[h][:])
+
+        def ov(h):
+            nc.vector.tensor_copy(oi[h][:].rearrange("p (c i) t -> p c t i", i=4), of[h][:].rearrange("p t (c i) -> p c t i", i=4))
+
+        def oq(h):
+            cols = slice(h * CH, (h + 1) * CH)
+            nc.vector.quantize_mx(out=o_codes[:, cols].bitcast(FP8X4), scales=o_scales[:, cols], in_=oi[h][:].rearrange("p n t -> p (n t)"))
+            nc.sync.dma_start(words_of(out_1)[:, cols], o_codes[:, cols].bitcast(I32))
+
+        ga(0)
+        th(0)
+        ga(1)
+        th(1)
+        zz(0)
+        zw(0)
+        ga(2)
+        th(2)
+        zq(0)
+        zz(1)
+        zw(1)
+        ow(0)
+        oe(0)
+        ga(3)
+        th(3)
+        zq(1)
+        zz(2)
+        zw(2)
+        oq(0)
+        ow(1)
+        oe(1)
+        zz(3)
+        zq(2)
+        zw(3)
+        oq(1)
+        zq(3)
+        oe(2)
+        oe(3)
+        ov(2)
+        ov(3)
+        oq(2)
+        oq(3)
+        for q in range(4):
+            (nc.sync, nc.scalar)[q % 2].dma_start(out_2[0, 4 * q : 4 * q + 4, :].bitcast(I32), o_scales[32 * q : 32 * q + 4, :].bitcast(I32))

@@ -16,26 +16,25 @@ P = 128
 PACK = 4
 K, T, S, H = 512, 2048, 512, 512
 FLOPS = 3 * 2 * K * H * S
-HALF = 256
-CH = 128
+HALF = S // 2
+CHUNK = 128
+LINE = 16
+OUT_SCALE = 0.0625
 
 
 def words_of(ap):
     return ap[0].rearrange("p n t -> p (n t)").bitcast(I32)
 
 
-def deal_words(eng, dst, src):
+def deal(eng, dst, src, per_line):
     eng.tensor_copy(
-        out=dst[:].bitcast(I32).rearrange("p (t c i) -> p c t i", t=PACK, i=4),
-        in_=src[:].bitcast(I32).rearrange("p (c i t) -> p c t i", t=PACK, i=4),
+        out=dst.rearrange("p (t c i) -> p c t i", t=PACK, i=per_line),
+        in_=src.rearrange("p (c i t) -> p c t i", t=PACK, i=per_line),
     )
 
 
-def deal_scales(eng, dst, src):
-    eng.tensor_copy(
-        out=dst[:].rearrange("p (t c i) -> p c t i", t=PACK, i=16),
-        in_=src[:].rearrange("p (c i t) -> p c t i", t=PACK, i=16),
-    )
+def weave_views(dst, src):
+    return dst.rearrange("p (c i) t -> p c t i", i=4), src.rearrange("p t (c i) -> p c t i", i=4)
 
 
 def tile_picked_symplec_none_po_kernel(
@@ -50,6 +49,9 @@ def tile_picked_symplec_none_po_kernel(
         def sb(name, shape, dtype, tag=None):
             return keep.tile(shape, dtype, name=name, tag=tag or name, align_bytes=64)
 
+        def slices(name, shape, dtype):
+            return [sb("%s_%d" % (name, n), shape, dtype) for n in range(PACK)]
+
         offs_t = keep.tile([P, S // 16], U16, name="offs_t")
         two_t = keep.tile([P, S // 16], U16, name="two_t")
         nb_t = keep.tile([P, S // 16], U16, name="nb_t")
@@ -62,238 +64,171 @@ def tile_picked_symplec_none_po_kernel(
         w2w = sb("w2w", [P, H], U32)
         w1s = sb("w1s", [P, H], U8)
         w2s = sb("w2s", [P, H], U8)
-        dsf = sb("dsf", [P, H], U8)
+        d_scale = sb("d_scale", [P, H], U8)
         gs_t = sb("gs_t", [P, PACK], F32)
         warm = sb("warm", [P, 8], F32)
 
         nc.vector.memset(xs[:].bitcast(I32), 0)
         nc.gpsimd.memset(warm[:], 0.0)
-        for tl in (w1s, w2s, ds, dsf):
+        for tl in (w1s, w2s, ds, d_scale):
             nc.vector.memset(tl[:].bitcast(I32), 0)
 
-        def load_scales(tl, src, eng):
+        def load_scales(tl, src):
             for q in range(4):
-                eng.dma_start(tl[32 * q : 32 * q + 4, :].bitcast(I32), src[0, 4 * q : 4 * q + 4, :].bitcast(I32))
+                nc.sync.dma_start(tl[32 * q : 32 * q + 4, :].bitcast(I32), src[0, 4 * q : 4 * q + 4, :].bitcast(I32))
 
         nc.sync.dma_start(offs_t[:], offs)
         nc.scalar.dma_start(w1w[:].bitcast(I32), words_of(w1_words))
-        nc.scalar.dma_start(gs_t[:], gs.rearrange("(p t) o -> p (t o)", t=PACK))
         nc.scalar.dma_start(xw[:].bitcast(I32), words_of(x_words))
         nc.scalar.activation(warm[:, 4:5], warm[:, 0:1], ACT.Tanh)
-        load_scales(xs, x_scales, nc.sync)
-        load_scales(w1s, w1_scales, nc.sync)
         nc.sync.dma_start(two_t[:], two)
-        nc.sync.dma_start(nb_t[:], nb)
-        nc.sync.dma_start(w2w[:].bitcast(I32), words_of(w2_words))
+        load_scales(xs, x_scales)
+        load_scales(w1s, w1_scales)
         nc.sync.dma_start(kq_t[:], kq)
         for e in range(2):
             nc.sync.dma_start(ds[e:P:16, :].bitcast(I32), d_scales[0, e:16:2, :].bitcast(I32))
-        load_scales(w2s, w2_scales, nc.gpsimd)
+        nc.sync.dma_start(nb_t[:], nb)
+        nc.sync.dma_start(w2w[:].bitcast(I32), words_of(w2_words))
+        load_scales(w2s, w2_scales)
+        nc.sync.dma_start(gs_t[:], gs.rearrange("(p t) o -> p (t o)", t=PACK))
         nc.sync.dma_start(dw[:].bitcast(I32), words_of(d_words))
 
-        xqs = sb("xqs", [P, S], U8)
-        x2s = sb("x2s", [P, S], U8)
-        xq = sb("xq", [P, S], U32)
-        x2 = sb("x2", [P, S], U32)
+        def product(acc, lw, ls, rw, rs, t):
+            m = slice(t * P, (t + 1) * P)
+            nc.tensor.matmul_mx(out=acc, lhsT=lw[:, m].bitcast(FP8X4), lhsT_scale=ls[:, m],
+                                rhs=rw[:].bitcast(FP8X4), rhs_scale=rs[:], start=True, stop=True)
+
+        xq_s = sb("xq_s", [P, S], U8)
+        x2_s = sb("x2_s", [P, S], U8)
         w1d = sb("w1d", [P, H], U32)
         w2d = sb("w2d", [P, H], U32)
         w1sd = sb("w1sd", [P, H], U8)
-        dd = sb("dd", [P, H], U32)
-        dsg = sb("dsg", [P, H], U8)
-        dsd = sb("dsd", [P, H], U8)
-
-        nc.vector.tensor_copy(xqs[:], xs[:].indirect(offs_t[:]))
-        deal_words(nc.vector, w1d, w1w)
-        deal_scales(nc.vector, w1sd, w1s)
-        nc.vector.tensor_copy(xq[:], xw[:].indirect(offs_t[:]))
-
-        def product(acc, lw, ls, rw, rs, t, cols):
-            m = slice(t * P, (t + 1) * P)
-            nc.tensor.matmul_mx(out=acc, lhsT=lw[:, m].bitcast(FP8X4), lhsT_scale=ls[:, m],
-                                rhs=rw[:, cols].bitcast(FP8X4), rhs_scale=rs[:, cols], start=True, stop=True)
-
-        full = slice(0, S)
+        w2sd = sb("w2sd", [P, H], U8)
+        nc.vector.tensor_copy(xq_s[:], xs[:].indirect(offs_t[:]))
+        nc.vector.tensor_copy(x2_s[:], xs[:].indirect(two_t[:]))
+        deal(nc.vector, w1d[:].bitcast(I32), w1w[:].bitcast(I32), LINE // 4)
+        deal(nc.vector, w1sd[:], w1s[:], LINE)
+        xq_w = sb("xq_w", [P, S], U32, tag="xs")
+        nc.vector.tensor_copy(xq_w[:], xw[:].indirect(offs_t[:]))
         y_ps = [psum.tile([P, S], F32, name="y_ps%d" % t, tag="a%d" % t) for t in range(PACK)]
         c_ps = [psum.tile([P, S], F32, name="c_ps%d" % t, tag="b%d" % t) for t in range(PACK)]
         for t in range(PACK):
-            product(y_ps[t][:], w1d, w1sd, xq, xqs, t, full)
-        nc.vector.tensor_copy(x2s[:], xs[:].indirect(two_t[:]))
-        nc.vector.tensor_copy(x2[:], xw[:].indirect(two_t[:]))
-        w2sd = sb("w2sd", [P, H], U8, tag="w1s")
-        deal_words(nc.vector, w2d, w2w)
-        deal_scales(nc.vector, w2sd, w2s)
+            product(y_ps[t][:], w1d, w1sd, xq_w, xq_s, t)
+        x2_w = sb("x2_w", [P, S], U32, tag="w1s")
+        nc.vector.tensor_copy(x2_w[:], xw[:].indirect(two_t[:]))
+        deal(nc.vector, w2d[:].bitcast(I32), w2w[:].bitcast(I32), LINE // 4)
+        deal(nc.vector, w2sd[:], w2s[:], LINE)
         for t in range(PACK):
-            product(c_ps[t][:], w2d, w2sd, x2, x2s, t, full)
-        nc.vector.tensor_copy(dsg[:], ds[:].indirect(kq_t[:]))
-        deal_scales(nc.vector, dsd, dsg)
-        for r, src in enumerate((0, 1, 16, 17)):
-            nc.sync.dma_start(dsf[r:P:32, :].bitcast(I32), dsd[src:P:32, :].bitcast(I32))
+            product(c_ps[t][:], w2d, w2sd, x2_w, x2_s, t)
 
-        def diff(dst, win, cp, lo, n):
-            nc.vector.tensor_tensor(dst, win[:].indirect(nb_t[:, lo // 16 : (lo + n) // 16]), cp[:, lo : lo + n], ALU.subtract)
+        ds_g = sb("ds_g", [P, H], U8)
+        ds_d = sb("ds_d", [P, H], U8)
+        nc.vector.tensor_copy(ds_g[:], ds[:].indirect(kq_t[:]))
+        deal(nc.vector, ds_d[:], ds_g[:], LINE)
+        for r in range(4):
+            src = 16 * (r // 2) + r % 2
+            nc.sync.dma_start(d_scale[r:P:32, :].bitcast(I32), ds_d[src:P:32, :].bitcast(I32))
 
-        y_win = [sb("y_win%d" % t, [P, S], F32) for t in range(PACK)]
-        y_cp = [sb("y_cp%d" % t, [P, S], F32) for t in range(PACK)]
-        g1 = [sb("g1_%d" % t, [P, S], F32) for t in range(PACK)]
-        t1 = [sb("t1_%d" % t, [P, S], F32) for t in range(PACK)]
-        vn = [sb("vn_%d" % t, [P, S], F32) for t in range(PACK)]
-        gvn = [sb("gvn_%d" % t, [P, S], F32) for t in range(PACK)]
-        x_win = [sb("x_win%d" % t, [P, S], F32) for t in range(PACK)]
-        x_cp = [sb("x_cp%d" % t, [P, S], F32) for t in range(PACK)]
+        wins = [sb("win%d" % k, [P, 2 * S], F32) for k in range(2 * PACK)]
+        last_twin = sb("last_twin", [P, S], F32)
+        nc.gpsimd.memset(wins[0][:, S:], 0.0)
+        val = [w[:, :S] for w in wins]
+        twin = [w[:, S:] for w in wins[1:]] + [last_twin[:]]
 
-        def pa(t):
-            nc.scalar.copy(y_win[t][:], y_ps[t][:])
+        def partner_minus_self(dst, k, lo, n):
+            offsets = nb_t[:, lo // 16 : (lo + n) // 16]
+            nc.vector.tensor_tensor(dst, wins[k][:].indirect(offsets), twin[k][:, lo : lo + n], ALU.subtract)
 
-        def pb(t):
-            nc.scalar.copy(y_cp[t][:], y_ps[t][:])
-
-        def p1(t):
-            for lo in range(0, S, HALF):
-                diff(g1[t][:, lo : lo + HALF], y_win[t], y_cp[t], lo, HALF)
-
-        def pt(t):
+        g1 = slices("g1", [P, S], F32)
+        t1 = slices("t1", [P, S], F32)
+        vn = slices("vn", [P, S], F32)
+        gvn = slices("gvn", [P, S], F32)
+        for t in range(PACK):
+            nc.scalar.copy(val[t], y_ps[t][:])
+            nc.scalar.copy(twin[t], y_ps[t][:])
+            partner_minus_self(g1[t][:], t, 0, S)
+        for t in range(PACK):
             nc.scalar.activation(t1[t][:], g1[t][:], ACT.Tanh)
-
-        def p2(t):
-            nc.vector.tensor_tensor(vn[t][:], t1[t][:], c_ps[t][:], ALU.add)
-
-        def p3(t):
-            nc.vector.scalar_tensor_tensor(x_win[t][:], vn[t][:], 0.5, y_cp[t][:], ALU.mult, ALU.add)
-
-        def p4(t):
-            nc.scalar.copy(x_cp[t][:], x_win[t][:])
-
-        def p5(t):
+        for t in range(PACK + 1):
+            if t < PACK:
+                nc.vector.tensor_tensor(vn[t][:], t1[t][:], c_ps[t][:], ALU.add)
+            if t > 0:
+                k = PACK + t - 1
+                nc.vector.scalar_tensor_tensor(val[k], vn[t - 1][:], 0.5, twin[t - 1], ALU.mult, ALU.add)
+                nc.scalar.copy(twin[k], val[k])
+        for t in range(PACK):
             nc.scalar.activation(gvn[t][:], vn[t][:], ACT.Copy, scale=gs_t[:, t : t + 1])
 
-        pa(0)
-        pb(0)
-        p1(0)
-        pa(1)
-        pb(1)
-        p1(1)
-        pa(2)
-        pt(0)
-        pb(2)
-        p2(0)
-        p1(2)
-        p3(0)
-        pt(1)
-        pa(3)
-        pb(3)
-        p2(1)
-        p1(3)
-        p3(1)
-        pt(2)
-        p4(0)
-        p5(0)
-        pt(3)
-        p2(2)
-        p2(3)
-        p3(2)
-        p3(3)
-        p4(1)
-        p5(1)
-        p4(2)
-        p5(2)
-        p4(3)
-        p5(3)
-        dg = sb("dg", [P, H], U32, tag="t1_3")
-        nc.vector.tensor_copy(dg[:], dw[:].indirect(kq_t[:]))
-        deal_words(nc.vector, dd, dg)
-
+        g2 = [slices("g2_%d" % u, [P, HALF], F32) for u in range(2)]
+        t2 = [slices("t2_%d" % u, [P, HALF], F32) for u in range(2)]
+        z = [sb("z_%d" % u, [P, PACK, HALF], BF16) for u in range(2)]
+        z_woven = slices("z_woven", [P, CHUNK, PACK], BF16)
+        z_w = slices("z_w", [P, CHUNK], U32)
+        z_s = slices("z_s", [P, CHUNK], U8)
+        o_f32 = slices("o_f32", [P, PACK, CHUNK], F32)
+        o_woven = slices("o_woven", [P, CHUNK, PACK], BF16)
+        o_w = sb("o_w", [P, S], U32)
+        o_s = sb("o_s", [P, S], U8)
+        d_dealt = sb("d_dealt", [P, H], U32)
         out_rows = out_0.rearrange("(p t) n -> p t n", t=PACK)
-        o_codes = sb("o_codes", [P, S], U32)
-        o_scales = sb("o_scales", [P, S], U8)
-        n_ch = S // CH
-        g2, t2 = {}, {}
-        zp = [sb("zp_%d" % h, [P, PACK, CH], BF16) for h in range(n_ch)]
-        zi = [sb("zi_%d" % h, [P, CH, PACK], BF16) for h in range(n_ch)]
-        zc = [sb("zc_%d" % h, [P, CH], U32) for h in range(n_ch)]
-        zs = [sb("zs_%d" % h, [P, CH], U8) for h in range(n_ch)]
-        of = [sb("of_%d" % h, [P, PACK, CH], F32) for h in range(n_ch)]
-        oi = [sb("oi_%d" % h, [P, CH, PACK], BF16) for h in range(n_ch)]
 
-        o_ps = {}
-
-        def ga(h):
-            g2[h] = sb("g2_%d" % h, [P, PACK, CH], F32, tag=("g1_3", "g1_2", "t2_0", "t2_1")[h])
+        def second_tanh(u):
             for t in range(PACK):
-                diff(g2[h][:, t, :], x_win[t], x_cp[t], h * CH, CH)
+                partner_minus_self(g2[u][t][:], PACK + t, u * HALF, HALF)
+                nc.scalar.activation(t2[u][t][:], g2[u][t][:], ACT.Tanh)
 
-        def th(h):
-            t2[h] = sb("t2_%d" % h, [P, PACK, CH], F32)
-            if h in ():
-                for t in range(PACK):
-                    nc.scalar.activation(t2[h][:, t, :], g2[h][:, t, :], ACT.Tanh)
-            else:
-                nc.scalar.activation(t2[h][:], g2[h][:], ACT.Tanh)
+        def make_z(u, t, lo, n):
+            nc.vector.scalar_tensor_tensor(z[u][:, t, lo : lo + n], t2[u][t][:, lo : lo + n], gs_t[:, t : t + 1],
+                                           gvn[t][:, u * HALF + lo : u * HALF + lo + n], ALU.mult, ALU.add)
 
-        def zz(h):
+        def z_views(h):
+            return weave_views(z_woven[h][:], z[h // 2][:, :, h % 2 * CHUNK : (h % 2 + 1) * CHUNK])
+
+        def last_product(h):
+            nc.vector.quantize_mx(out=z_w[h][:].bitcast(FP8X4), scales=z_s[h][:],
+                                  in_=z_woven[h][:].rearrange("p n t -> p (n t)"))
+            acc = psum.tile([P, PACK, CHUNK], F32, name="o_ps%d" % h, tag="a%d" % h)
             for t in range(PACK):
-                nc.vector.scalar_tensor_tensor(zp[h][:, t, :], t2[h][:, t, :], gs_t[:, t : t + 1],
-                                               gvn[t][:, h * CH : (h + 1) * CH], ALU.mult, ALU.add)
+                product(acc[:, t, :], d_dealt, d_scale, z_w[h], z_s[h], t)
+            return acc
 
-        def zw(h):
-            dst = zi[h][:].rearrange("p (c i) t -> p c t i", i=4)
-            src = zp[h][:].rearrange("p t (c i) -> p c t i", i=4)
-            if h in (3,):
-                nc.vector.tensor_copy(dst, src)
-            else:
-                nc.scalar.copy(dst, src)
+        def store_f32(h, acc):
+            nc.scalar.activation(o_f32[h][:], acc[:], ACT.Copy, scale=OUT_SCALE)
+            nc.sync.dma_start(out_rows[:, :, h * CHUNK : (h + 1) * CHUNK], o_f32[h][:])
 
-        def zq(h):
-            nc.vector.quantize_mx(out=zc[h][:].bitcast(FP8X4), scales=zs[h][:], in_=zi[h][:].rearrange("p n t -> p (n t)"))
-            o_ps[h] = psum.tile([P, PACK, CH], F32, name="o_ps%d" % h, tag="a%d" % h)
-            for t in range(PACK):
-                product(o_ps[h][:, t, :], dd, dsf, zc[h], zs[h], t, slice(0, CH))
+        def make_planes(h):
+            cols = slice(h * CHUNK, (h + 1) * CHUNK)
+            nc.vector.quantize_mx(out=o_w[:, cols].bitcast(FP8X4), scales=o_s[:, cols],
+                                  in_=o_woven[h][:].rearrange("p n t -> p (n t)"))
+            if h % 2:
+                cols = slice((h - 1) * CHUNK, (h + 1) * CHUNK)
+                nc.sync.dma_start(words_of(out_1)[:, cols], o_w[:, cols].bitcast(I32))
 
-        def ow(h):
-            nc.scalar.activation(oi[h][:], o_ps[h][:].rearrange("p t n -> p n t"), ACT.Copy, scale=0.0625)
+        second_tanh(0)
+        d_g = sb("d_g", [P, H], U32, tag="t1_%d" % (PACK - 1))
+        nc.vector.tensor_copy(d_g[:], dw[:].indirect(kq_t[:]))
+        for t in range(PACK):
+            make_z(0, t, 0, HALF)
+        for h in (0, 1):
+            nc.scalar.copy(*z_views(h))
+        deal(nc.vector, d_dealt[:].bitcast(I32), d_g[:].bitcast(I32), LINE // 4)
+        second_tanh(1)
+        for h in (0, 1):
+            acc = last_product(h)
+            nc.scalar.activation(o_woven[h][:], acc[:].rearrange("p t n -> p n t"), ACT.Copy, scale=OUT_SCALE)
+            store_f32(h, acc)
 
-        def oe(h):
-            nc.scalar.activation(of[h][:], o_ps[h][:], ACT.Copy, scale=0.0625)
-            nc.sync.dma_start(out_rows[:, :, h * CH : (h + 1) * CH], of[h][:])
-
-        def ov(h):
-            nc.vector.tensor_copy(oi[h][:].rearrange("p (c i) t -> p c t i", i=4), of[h][:].rearrange("p t (c i) -> p c t i", i=4))
-
-        def oq(h):
-            cols = slice(h * CH, (h + 1) * CH)
-            nc.vector.quantize_mx(out=o_codes[:, cols].bitcast(FP8X4), scales=o_scales[:, cols], in_=oi[h][:].rearrange("p n t -> p (n t)"))
-            nc.sync.dma_start(words_of(out_1)[:, cols], o_codes[:, cols].bitcast(I32))
-
-        ga(0)
-        th(0)
-        ga(1)
-        th(1)
-        zz(0)
-        zw(0)
-        ga(2)
-        th(2)
-        zq(0)
-        zz(1)
-        zw(1)
-        ow(0)
-        oe(0)
-        ga(3)
-        th(3)
-        zq(1)
-        zz(2)
-        zw(2)
-        oq(0)
-        ow(1)
-        oe(1)
-        zz(3)
-        zq(2)
-        zw(3)
-        oq(1)
-        zq(3)
-        oe(2)
-        oe(3)
-        ov(2)
-        ov(3)
-        oq(2)
-        oq(3)
+        for t in range(PACK - 1):
+            make_z(1, t, 0, HALF)
+        for h in (2, 3):
+            make_z(1, PACK - 1, h % 2 * CHUNK, CHUNK)
+            nc.vector.tensor_copy(*z_views(h))
+            store_f32(h, last_product(h))
+        for h in (0, 1):
+            make_planes(h)
+        for h in (2, 3):
+            nc.vector.tensor_copy(*weave_views(o_woven[h][:], o_f32[h][:]))
+            make_planes(h)
         for q in range(4):
-            (nc.sync, nc.scalar)[q % 2].dma_start(out_2[0, 4 * q : 4 * q + 4, :].bitcast(I32), o_scales[32 * q : 32 * q + 4, :].bitcast(I32))
+            queue = (nc.sync, nc.scalar)[q % 2]
+            queue.dma_start(out_2[0, 4 * q : 4 * q + 4, :].bitcast(I32), o_s[32 * q : 32 * q + 4, :].bitcast(I32))

@@ -68,25 +68,25 @@ def tile_picked_symplec_none_po_kernel(
         gs_t = sb("gs_t", [P, PACK], F32)
         warm = sb("warm", [P, 8], F32)
 
-        nc.vector.memset(xs[:].bitcast(I32), 0)
+        for tl in (xs, w1s):
+            nc.gpsimd.memset(tl[:].bitcast(I32), 0)
         nc.gpsimd.memset(warm[:], 0.0)
-        for tl in (w1s, w2s, ds, d_scale):
-            nc.vector.memset(tl[:].bitcast(I32), 0)
+        for tl in (w2s, d_scale):
+            nc.gpsimd.memset(tl[:].bitcast(I32), 0)
 
         def load_scales(tl, src):
             for q in range(4):
                 nc.sync.dma_start(tl[32 * q : 32 * q + 4, :].bitcast(I32), src[0, 4 * q : 4 * q + 4, :].bitcast(I32))
 
-        nc.sync.dma_start(offs_t[:], offs)
-        nc.scalar.dma_start(w1w[:].bitcast(I32), words_of(w1_words))
-        nc.scalar.dma_start(xw[:].bitcast(I32), words_of(x_words))
         nc.scalar.activation(warm[:, 4:5], warm[:, 0:1], ACT.Tanh)
-        nc.sync.dma_start(two_t[:], two)
+        nc.sync.dma_start(w1w[:].bitcast(I32), words_of(w1_words))
+        nc.sync.dma_start(offs_t[:], offs)
         load_scales(xs, x_scales)
+        nc.sync.dma_start(two_t[:], two)
+        nc.sync.dma_start(xw[:].bitcast(I32), words_of(x_words))
         load_scales(w1s, w1_scales)
         nc.sync.dma_start(kq_t[:], kq)
-        for e in range(2):
-            nc.sync.dma_start(ds[e:P:16, :].bitcast(I32), d_scales[0, e:16:2, :].bitcast(I32))
+        nc.sync.dma_start(ds[:].bitcast(I32), d_scales[0].bitcast(I32).unsqueeze(1).to_broadcast([16, 8, T // 4]))
         nc.sync.dma_start(nb_t[:], nb)
         nc.sync.dma_start(w2w[:].bitcast(I32), words_of(w2_words))
         load_scales(w2s, w2_scales)
@@ -108,7 +108,7 @@ def tile_picked_symplec_none_po_kernel(
         nc.vector.tensor_copy(x2_s[:], xs[:].indirect(two_t[:]))
         deal(nc.vector, w1d[:].bitcast(I32), w1w[:].bitcast(I32), LINE // 4)
         deal(nc.vector, w1sd[:], w1s[:], LINE)
-        xq_w = sb("xq_w", [P, S], U32, tag="xs")
+        xq_w = sb("xq_w", [P, S], U32)
         nc.vector.tensor_copy(xq_w[:], xw[:].indirect(offs_t[:]))
         y_ps = [psum.tile([P, S], F32, name="y_ps%d" % t, tag="a%d" % t) for t in range(PACK)]
         c_ps = [psum.tile([P, S], F32, name="c_ps%d" % t, tag="b%d" % t) for t in range(PACK)]
@@ -122,12 +122,11 @@ def tile_picked_symplec_none_po_kernel(
             product(c_ps[t][:], w2d, w2sd, x2_w, x2_s, t)
 
         ds_g = sb("ds_g", [P, H], U8)
-        ds_d = sb("ds_d", [P, H], U8)
+        ds_d = sb("ds_d", [P, H], U8, tag="w2s")
         nc.vector.tensor_copy(ds_g[:], ds[:].indirect(kq_t[:]))
         deal(nc.vector, ds_d[:], ds_g[:], LINE)
         for r in range(4):
-            src = 16 * (r // 2) + r % 2
-            nc.sync.dma_start(d_scale[r:P:32, :].bitcast(I32), ds_d[src:P:32, :].bitcast(I32))
+            nc.sync.dma_start(d_scale[r:P:32, :].bitcast(I32), ds_d[8 * r : P : 32, :].bitcast(I32))
 
         wins = [sb("win%d" % k, [P, 2 * S], F32) for k in range(2 * PACK)]
         last_twin = sb("last_twin", [P, S], F32)

@@ -20,6 +20,8 @@ HALF = S // 2
 CHUNK = 128
 LINE = 16
 OUT_SCALE = 0.0625
+G2T = (0, 1, 2, 3)
+GVT = (0, 1)
 
 
 def words_of(ap):
@@ -122,11 +124,7 @@ def tile_picked_symplec_none_po_kernel(
             product(c_ps[t][:], w2d, w2sd, x2_w, x2_s, t)
 
         ds_g = sb("ds_g", [P, H], U8)
-        ds_d = sb("ds_d", [P, H], U8, tag="w2s")
         nc.vector.tensor_copy(ds_g[:], ds[:].indirect(kq_t[:]))
-        deal(nc.vector, ds_d[:], ds_g[:], LINE)
-        for r in range(4):
-            nc.sync.dma_start(d_scale[r:P:32, :].bitcast(I32), ds_d[8 * r : P : 32, :].bitcast(I32))
 
         wins = [sb("win%d" % k, [P, 2 * S], F32) for k in range(2 * PACK)]
         last_twin = sb("last_twin", [P, S], F32)
@@ -141,24 +139,36 @@ def tile_picked_symplec_none_po_kernel(
         g1 = slices("g1", [P, S], F32)
         t1 = slices("t1", [P, S], F32)
         vn = slices("vn", [P, S], F32)
-        gvn = slices("gvn", [P, S], F32)
+        gvn = {}
         for t in range(PACK):
-            nc.scalar.copy(val[t], y_ps[t][:])
-            nc.scalar.copy(twin[t], y_ps[t][:])
+            nc.scalar.activation(val[t], y_ps[t][:], ACT.Copy, scale=2.0)
+            nc.scalar.activation(twin[t], y_ps[t][:], ACT.Copy, scale=2.0)
             partner_minus_self(g1[t][:], t, 0, S)
         for t in range(PACK):
-            nc.scalar.activation(t1[t][:], g1[t][:], ACT.Tanh)
-        for t in range(PACK + 1):
-            if t < PACK:
-                nc.vector.tensor_tensor(vn[t][:], t1[t][:], c_ps[t][:], ALU.add)
-            if t > 0:
-                k = PACK + t - 1
-                nc.vector.scalar_tensor_tensor(val[k], vn[t - 1][:], 0.5, twin[t - 1], ALU.mult, ALU.add)
-                nc.scalar.copy(twin[k], val[k])
+            nc.scalar.activation(t1[t][:], g1[t][:], ACT.Tanh, scale=0.5)
+        ds_d = sb("ds_d", [P, H], U8, tag="g1_0")
+        deal(nc.vector, ds_d[:], ds_g[:], LINE)
+        for r in range(4):
+            nc.sync.dma_start(d_scale[r:P:32, :].bitcast(I32), ds_d[8 * r : P : 32, :].bitcast(I32))
+
         for t in range(PACK):
+            nc.vector.tensor_tensor(vn[t][:], t1[t][:], c_ps[t][:], ALU.add)
+        for t in range(PACK):
+            k = PACK + t
+            if t < 2:
+                nc.gpsimd.tensor_tensor(val[k], vn[t][:], val[t], ALU.add)
+            else:
+                nc.vector.scalar_tensor_tensor(val[k], y_ps[t][:], 2.0, vn[t][:], ALU.mult, ALU.add)
+            nc.scalar.copy(twin[k], val[k])
+
+        def weigh(t, tag):
+            gvn[t] = sb("gvn_%d" % t, [P, S], F32, tag=tag)
             nc.scalar.activation(gvn[t][:], vn[t][:], ACT.Copy, scale=gs_t[:, t : t + 1])
 
-        g2 = [slices("g2_%d" % u, [P, HALF], F32) for u in range(2)]
+        for t in range(PACK):
+            weigh(t, None)
+
+        g2 = [slices("g2_0", [P, HALF], F32), {}]
         t2 = [slices("t2_%d" % u, [P, HALF], F32) for u in range(2)]
         z = [sb("z_%d" % u, [P, PACK, HALF], BF16) for u in range(2)]
         z_woven = slices("z_woven", [P, CHUNK, PACK], BF16)
@@ -168,13 +178,14 @@ def tile_picked_symplec_none_po_kernel(
         o_woven = slices("o_woven", [P, CHUNK, PACK], BF16)
         o_w = sb("o_w", [P, S], U32)
         o_s = sb("o_s", [P, S], U8)
-        d_dealt = sb("d_dealt", [P, H], U32)
         out_rows = out_0.rearrange("(p t) n -> p t n", t=PACK)
 
         def second_tanh(u):
             for t in range(PACK):
+                if u:
+                    g2[u][t] = sb("g2_1_%d" % t, [P, HALF], F32, tag="t2_0_%d" % G2T[t])
                 partner_minus_self(g2[u][t][:], PACK + t, u * HALF, HALF)
-                nc.scalar.activation(t2[u][t][:], g2[u][t][:], ACT.Tanh)
+                nc.scalar.activation(t2[u][t][:], g2[u][t][:], ACT.Tanh, scale=0.5)
 
         def make_z(u, t, lo, n):
             nc.vector.scalar_tensor_tensor(z[u][:, t, lo : lo + n], t2[u][t][:, lo : lo + n], gs_t[:, t : t + 1],
@@ -206,6 +217,7 @@ def tile_picked_symplec_none_po_kernel(
         second_tanh(0)
         d_g = sb("d_g", [P, H], U32, tag="t1_%d" % (PACK - 1))
         nc.vector.tensor_copy(d_g[:], dw[:].indirect(kq_t[:]))
+        d_dealt = sb("d_dealt", [P, H], U32, tag="g2_0_0")
         for t in range(PACK):
             make_z(0, t, 0, HALF)
         for h in (0, 1):
@@ -214,7 +226,8 @@ def tile_picked_symplec_none_po_kernel(
         second_tanh(1)
         for h in (0, 1):
             acc = last_product(h)
-            nc.scalar.activation(o_woven[h][:], acc[:].rearrange("p t n -> p n t"), ACT.Copy, scale=OUT_SCALE)
+            if h in GVT:
+                nc.scalar.activation(o_woven[h][:], acc[:].rearrange("p t n -> p n t"), ACT.Copy, scale=OUT_SCALE)
             store_f32(h, acc)
 
         for t in range(PACK - 1):
@@ -223,10 +236,9 @@ def tile_picked_symplec_none_po_kernel(
             make_z(1, PACK - 1, h % 2 * CHUNK, CHUNK)
             nc.vector.tensor_copy(*z_views(h))
             store_f32(h, last_product(h))
-        for h in (0, 1):
-            make_planes(h)
-        for h in (2, 3):
-            nc.vector.tensor_copy(*weave_views(o_woven[h][:], o_f32[h][:]))
+        for h in range(PACK):
+            if h not in GVT:
+                nc.vector.tensor_copy(*weave_views(o_woven[h][:], o_f32[h][:]))
             make_planes(h)
         for q in range(4):
             queue = (nc.sync, nc.scalar)[q % 2]

@@ -16,6 +16,7 @@ P = 128
 PACK = 4
 K, T, S, H = 512, 2048, 512, 512
 FLOPS = 3 * 2 * K * H * S
+POOL_COLS = 1280
 HALF = S // 2
 CHUNK = 128
 LINE = 16
@@ -89,8 +90,8 @@ def tile_picked_symplec_none_po_kernel(
         load_scales(w1s, w1_scales)
         nc.sync.dma_start(kq_t[:], kq)
         nc.sync.dma_start(ds[:].bitcast(I32), d_scales[0].bitcast(I32).unsqueeze(1).to_broadcast([16, 8, T // 4]))
-        nc.sync.dma_start(nb_t[:], nb)
         nc.sync.dma_start(w2w[:].bitcast(I32), words_of(w2_words))
+        nc.sync.dma_start(nb_t[:], nb)
         load_scales(w2s, w2_scales)
         nc.sync.dma_start(gs_t[:], gs.rearrange("(p t) o -> p (t o)", t=PACK))
         nc.sync.dma_start(dw[:].bitcast(I32), words_of(d_words))
@@ -109,17 +110,17 @@ def tile_picked_symplec_none_po_kernel(
         nc.vector.tensor_copy(xq_s[:], xs[:].indirect(offs_t[:]))
         nc.vector.tensor_copy(x2_s[:], xs[:].indirect(two_t[:]))
         deal(nc.vector, w1d[:].bitcast(I32), w1w[:].bitcast(I32), LINE // 4)
-        deal(nc.vector, w1sd[:], w1s[:], LINE)
+        deal(nc.gpsimd, w1sd[:], w1s[:], LINE)
         xq_w = sb("xq_w", [P, S], U32)
         nc.vector.tensor_copy(xq_w[:], xw[:].indirect(offs_t[:]))
         y_ps = [psum.tile([P, S], F32, name="y_ps%d" % t, tag="a%d" % t) for t in range(PACK)]
         c_ps = [psum.tile([P, S], F32, name="c_ps%d" % t, tag="b%d" % t) for t in range(PACK)]
         for t in range(PACK):
             product(y_ps[t][:], w1d, w1sd, xq_w, xq_s, t)
-        x2_w = sb("x2_w", [P, S], U32, tag="w1s")
+        x2_w = sb("x2_w", [P, S], U32)
         nc.vector.tensor_copy(x2_w[:], xw[:].indirect(two_t[:]))
-        deal(nc.vector, w2d[:].bitcast(I32), w2w[:].bitcast(I32), LINE // 4)
-        deal(nc.vector, w2sd[:], w2s[:], LINE)
+        deal(nc.gpsimd, w2d[:].bitcast(I32), w2w[:].bitcast(I32), LINE // 4)
+        deal(nc.gpsimd, w2sd[:], w2s[:], LINE)
         for t in range(PACK):
             product(c_ps[t][:], w2d, w2sd, x2_w, x2_s, t)
 
@@ -146,19 +147,15 @@ def tile_picked_symplec_none_po_kernel(
             partner_minus_self(g1[t][:], t, 0, S)
         for t in range(PACK):
             nc.scalar.activation(t1[t][:], g1[t][:], ACT.Tanh, scale=0.5)
-        ds_d = sb("ds_d", [P, H], U8, tag="g1_0")
-        deal(nc.vector, ds_d[:], ds_g[:], LINE)
-        for r in range(4):
-            nc.sync.dma_start(d_scale[r:P:32, :].bitcast(I32), ds_d[8 * r : P : 32, :].bitcast(I32))
-
         for t in range(PACK):
             nc.vector.tensor_tensor(vn[t][:], t1[t][:], c_ps[t][:], ALU.add)
         for t in range(PACK):
             k = PACK + t
-            if t < 2:
-                nc.gpsimd.tensor_tensor(val[k], vn[t][:], val[t], ALU.add)
-            else:
-                nc.vector.scalar_tensor_tensor(val[k], y_ps[t][:], 2.0, vn[t][:], ALU.mult, ALU.add)
+            n = min(max(POOL_COLS - t * S, 0), S)
+            if n:
+                nc.gpsimd.tensor_tensor(val[k][:, :n], vn[t][:, :n], val[t][:, :n], ALU.add)
+            if n < S:
+                nc.vector.scalar_tensor_tensor(val[k][:, n:], y_ps[t][:, n:], 2.0, vn[t][:, n:], ALU.mult, ALU.add)
             nc.scalar.copy(twin[k], val[k])
 
         def weigh(t, tag):
@@ -214,10 +211,15 @@ def tile_picked_symplec_none_po_kernel(
                 cols = slice((h - 1) * CHUNK, (h + 1) * CHUNK)
                 nc.sync.dma_start(words_of(out_1)[:, cols], o_w[:, cols].bitcast(I32))
 
-        second_tanh(0)
         d_g = sb("d_g", [P, H], U32, tag="t1_%d" % (PACK - 1))
         nc.vector.tensor_copy(d_g[:], dw[:].indirect(kq_t[:]))
-        d_dealt = sb("d_dealt", [P, H], U32, tag="g2_0_0")
+        second_tanh(0)
+        ds_d = sb("ds_d", [P, H], U8, tag="g2_0_0")
+        deal(nc.vector, ds_d[:], ds_g[:], LINE)
+        for r in range(4):
+            nc.sync.dma_start(d_scale[r:P:32, :].bitcast(I32), ds_d[8 * r : P : 32, :].bitcast(I32))
+
+        d_dealt = sb("d_dealt", [P, H], U32, tag="g2_0_1")
         for t in range(PACK):
             make_z(0, t, 0, HALF)
         for h in (0, 1):
@@ -235,7 +237,10 @@ def tile_picked_symplec_none_po_kernel(
         for h in (2, 3):
             make_z(1, PACK - 1, h % 2 * CHUNK, CHUNK)
             nc.vector.tensor_copy(*z_views(h))
-            store_f32(h, last_product(h))
+            acc = last_product(h)
+            if h in GVT:
+                nc.scalar.activation(o_woven[h][:], acc[:].rearrange("p t n -> p n t"), ACT.Copy, scale=OUT_SCALE)
+            store_f32(h, acc)
         for h in range(PACK):
             if h not in GVT:
                 nc.vector.tensor_copy(*weave_views(o_woven[h][:], o_f32[h][:]))

from contextlib import ExitStack

import concourse.mybir as mybir

F32 = mybir.dt.float32
BF16 = mybir.dt.bfloat16
I32 = mybir.dt.int32
U32 = mybir.dt.uint32
U16 = mybir.dt.uint16
U8 = mybir.dt.uint8
FP8X4 = mybir.dt.float8_e4m3fn_x4
ACT = mybir.ActivationFunctionType
ALU = mybir.AluOpType

P = 128
PACK = 4
K, T, S, H = 512, 2048, 512, 512
FLOPS = 3 * 2 * K * H * S
POOL_COLS = 1280
HALF = S // 2
CHUNK = 128
LINE = 16
OUT_SCALE = 0.0625
G2T = (0, 1, 2, 3)
GVT = (0, 1)


def words_of(ap):
    return ap[0].rearrange("p n t -> p (n t)").bitcast(I32)


def deal(eng, dst, src, per_line):
    eng.tensor_copy(
        out=dst.rearrange("p (t c i) -> p c t i", t=PACK, i=per_line),
        in_=src.rearrange("p (c i t) -> p c t i", t=PACK, i=per_line),
    )


def weave_views(dst, src):
    return dst.rearrange("p (c i) t -> p c t i", i=4), src.rearrange("p t (c i) -> p c t i", i=4)


def tile_picked_symplec_none_po_kernel(
    tc, x_words, x_scales, w1_words, w1_scales, w2_words, w2_scales, gs, d_words, d_scales,
    offs, two, nb, kq, out_0, out_1, out_2,
):
    nc = tc.nc
    with ExitStack() as ctx:
        keep = ctx.enter_context(tc.tile_pool(name="keep", bufs=1))
        psum = ctx.enter_context(tc.psum_pool(name="psum", bufs=1))

        def sb(name, shape, dtype, tag=None):
            return keep.tile(shape, dtype, name=name, tag=tag or name, align_bytes=64)

        def slices(name, shape, dtype):
            return [sb("%s_%d" % (name, n), shape, dtype) for n in range(PACK)]

        offs_t = keep.tile([P, S // 16], U16, name="offs_t")
        two_t = keep.tile([P, S // 16], U16, name="two_t")
        nb_t = keep.tile([P, S // 16], U16, name="nb_t")
        kq_t = keep.tile([P, H // 16], U16, name="kq_t")
        xw = sb("xw", [P, T], U32)
        xs = sb("xs", [P, T], U8)
        dw = sb("dw", [P, T], U32)
        ds = sb("ds", [P, T], U8)
        w1w = sb("w1w", [P, H], U32)
        w2w = sb("w2w", [P, H], U32)
        w1s = sb("w1s", [P, H], U8)
        w2s = sb("w2s", [P, H], U8)
        d_scale = sb("d_scale", [P, H], U8)
        gs_t = sb("gs_t", [P, PACK], F32)
        warm = sb("warm", [P, 8], F32)

        for tl in (xs, w1s):
            nc.gpsimd.memset(tl[:].bitcast(I32), 0)
        nc.gpsimd.memset(warm[:], 0.0)
        for tl in (w2s, d_scale):
            nc.gpsimd.memset(tl[:].bitcast(I32), 0)

        def load_scales(tl, src):
            for q in range(4):
                nc.sync.dma_start(tl[32 * q : 32 * q + 4, :].bitcast(I32), src[0, 4 * q : 4 * q + 4, :].bitcast(I32))

        nc.scalar.activation(warm[:, 4:5], warm[:, 0:1], ACT.Tanh)
        nc.sync.dma_start(w1w[:].bitcast(I32), words_of(w1_words))
        nc.sync.dma_start(offs_t[:], offs)
        load_scales(xs, x_scales)
        nc.sync.dma_start(two_t[:], two)
        nc.sync.dma_start(xw[:].bitcast(I32), words_of(x_words))
        load_scales(w1s, w1_scales)
        nc.sync.dma_start(kq_t[:], kq)
        nc.sync.dma_start(ds[:].bitcast(I32), d_scales[0].bitcast(I32).unsqueeze(1).to_broadcast([16, 8, T // 4]))
        nc.sync.dma_start(w2w[:].bitcast(I32), words_of(w2_words))
        nc.sync.dma_start(nb_t[:], nb)
        load_scales(w2s, w2_scales)
        nc.sync.dma_start(gs_t[:], gs.rearrange("(p t) o -> p (t o)", t=PACK))
        nc.sync.dma_start(dw[:].bitcast(I32), words_of(d_words))

        def product(acc, lw, ls, rw, rs, t):
            m = slice(t * P, (t + 1) * P)
            nc.tensor.matmul_mx(out=acc, lhsT=lw[:, m].bitcast(FP8X4), lhsT_scale=ls[:, m],
                                rhs=rw[:].bitcast(FP8X4), rhs_scale=rs[:], start=True, stop=True)

        xq_s = sb("xq_s", [P, S], U8)
        x2_s = sb("x2_s", [P, S], U8)
        w1d = sb("w1d", [P, H], U32)
        w2d = sb("w2d", [P, H], U32)
        w1sd = sb("w1sd", [P, H], U8)
        w2sd = sb("w2sd", [P, H], U8)
        nc.vector.tensor_copy(xq_s[:], xs[:].indirect(offs_t[:]))
        nc.vector.tensor_copy(x2_s[:], xs[:].indirect(two_t[:]))
        deal(nc.vector, w1d[:].bitcast(I32), w1w[:].bitcast(I32), LINE // 4)
        deal(nc.gpsimd, w1sd[:], w1s[:], LINE)
        xq_w = sb("xq_w", [P, S], U32)
        nc.vector.tensor_copy(xq_w[:], xw[:].indirect(offs_t[:]))
        y_ps = [psum.tile([P, S], F32, name="y_ps%d" % t, tag="a%d" % t) for t in range(PACK)]
        c_ps = [psum.tile([P, S], F32, name="c_ps%d" % t, tag="b%d" % t) for t in range(PACK)]
        for t in range(PACK):
            product(y_ps[t][:], w1d, w1sd, xq_w, xq_s, t)
        x2_w = sb("x2_w", [P, S], U32)
        nc.vector.tensor_copy(x2_w[:], xw[:].indirect(two_t[:]))
        deal(nc.gpsimd, w2d[:].bitcast(I32), w2w[:].bitcast(I32), LINE // 4)
        deal(nc.gpsimd, w2sd[:], w2s[:], LINE)
        for t in range(PACK):
            product(c_ps[t][:], w2d, w2sd, x2_w, x2_s, t)

        ds_g = sb("ds_g", [P, H], U8)
        nc.vector.tensor_copy(ds_g[:], ds[:].indirect(kq_t[:]))

        wins = [sb("win%d" % k, [P, 2 * S], F32) for k in range(2 * PACK)]
        last_twin = sb("last_twin", [P, S], F32)
        nc.gpsimd.memset(wins[0][:, S:], 0.0)
        val = [w[:, :S] for w in wins]
        twin = [w[:, S:] for w in wins[1:]] + [last_twin[:]]

        def partner_minus_self(dst, k, lo, n):
            offsets = nb_t[:, lo // 16 : (lo + n) // 16]
            nc.vector.tensor_tensor(dst, wins[k][:].indirect(offsets), twin[k][:, lo : lo + n], ALU.subtract)

        g1 = slices("g1", [P, S], F32)
        t1 = slices("t1", [P, S], F32)
        vn = slices("vn", [P, S], F32)
        gvn = {}
        for t in range(PACK):
            nc.scalar.activation(val[t], y_ps[t][:], ACT.Copy, scale=2.0)
            nc.scalar.activation(twin[t], y_ps[t][:], ACT.Copy, scale=2.0)
            partner_minus_self(g1[t][:], t, 0, S)
        for t in range(PACK):
            nc.scalar.activation(t1[t][:], g1[t][:], ACT.Tanh, scale=0.5)
        for t in range(PACK):
            nc.vector.tensor_tensor(vn[t][:], t1[t][:], c_ps[t][:], ALU.add)
        for t in range(PACK):
            k = PACK + t
            n = min(max(POOL_COLS - t * S, 0), S)
            if n:
                nc.gpsimd.tensor_tensor(val[k][:, :n], vn[t][:, :n], val[t][:, :n], ALU.add)
            if n < S:
                nc.vector.scalar_tensor_tensor(val[k][:, n:], y_ps[t][:, n:], 2.0, vn[t][:, n:], ALU.mult, ALU.add)
            nc.scalar.copy(twin[k], val[k])

        def weigh(t, tag):
            gvn[t] = sb("gvn_%d" % t, [P, S], F32, tag=tag)
            nc.scalar.activation(gvn[t][:], vn[t][:], ACT.Copy, scale=gs_t[:, t : t + 1])

        for t in range(PACK):
            weigh(t, None)

        g2 = [slices("g2_0", [P, HALF], F32), {}]
        t2 = [slices("t2_%d" % u, [P, HALF], F32) for u in range(2)]
        z = [sb("z_%d" % u, [P, PACK, HALF], BF16) for u in range(2)]
        z_woven = slices("z_woven", [P, CHUNK, PACK], BF16)
        z_w = slices("z_w", [P, CHUNK], U32)
        z_s = slices("z_s", [P, CHUNK], U8)
        o_f32 = slices("o_f32", [P, PACK, CHUNK], F32)
        o_woven = slices("o_woven", [P, CHUNK, PACK], BF16)
        o_w = sb("o_w", [P, S], U32)
        o_s = sb("o_s", [P, S], U8)
        out_rows = out_0.rearrange("(p t) n -> p t n", t=PACK)

        def second_tanh(u):
            for t in range(PACK):
                if u:
                    g2[u][t] = sb("g2_1_%d" % t, [P, HALF], F32, tag="t2_0_%d" % G2T[t])
                partner_minus_self(g2[u][t][:], PACK + t, u * HALF, HALF)
                nc.scalar.activation(t2[u][t][:], g2[u][t][:], ACT.Tanh, scale=0.5)

        def make_z(u, t, lo, n):
            nc.vector.scalar_tensor_tensor(z[u][:, t, lo : lo + n], t2[u][t][:, lo : lo + n], gs_t[:, t : t + 1],
                                           gvn[t][:, u * HALF + lo : u * HALF + lo + n], ALU.mult, ALU.add)

        def z_views(h):
            return weave_views(z_woven[h][:], z[h // 2][:, :, h % 2 * CHUNK : (h % 2 + 1) * CHUNK])

        def last_product(h):
            nc.vector.quantize_mx(out=z_w[h][:].bitcast(FP8X4), scales=z_s[h][:],
                                  in_=z_woven[h][:].rearrange("p n t -> p (n t)"))
            acc = psum.tile([P, PACK, CHUNK], F32, name="o_ps%d" % h, tag="a%d" % h)
            for t in range(PACK):
                product(acc[:, t, :], d_dealt, d_scale, z_w[h], z_s[h], t)
            return acc

        def store_f32(h, acc):
            nc.scalar.activation(o_f32[h][:], acc[:], ACT.Copy, scale=OUT_SCALE)
            nc.sync.dma_start(out_rows[:, :, h * CHUNK : (h + 1) * CHUNK], o_f32[h][:])

        def make_planes(h):
            cols = slice(h * CHUNK, (h + 1) * CHUNK)
            nc.vector.quantize_mx(out=o_w[:, cols].bitcast(FP8X4), scales=o_s[:, cols],
                                  in_=o_woven[h][:].rearrange("p n t -> p (n t)"))
            if h % 2:
                cols = slice((h - 1) * CHUNK, (h + 1) * CHUNK)
                nc.sync.dma_start(words_of(out_1)[:, cols], o_w[:, cols].bitcast(I32))

        d_g = sb("d_g", [P, H], U32, tag="t1_%d" % (PACK - 1))
        nc.vector.tensor_copy(d_g[:], dw[:].indirect(kq_t[:]))
        second_tanh(0)
        ds_d = sb("ds_d", [P, H], U8, tag="g2_0_0")
        deal(nc.vector, ds_d[:], ds_g[:], LINE)
        for r in range(4):
            nc.sync.dma_start(d_scale[r:P:32, :].bitcast(I32), ds_d[8 * r : P : 32, :].bitcast(I32))

        d_dealt = sb("d_dealt", [P, H], U32, tag="g2_0_1")
        for t in range(PACK):
            make_z(0, t, 0, HALF)
        for h in (0, 1):
            nc.scalar.copy(*z_views(h))
        deal(nc.vector, d_dealt[:].bitcast(I32), d_g[:].bitcast(I32), LINE // 4)
        second_tanh(1)
        for h in (0, 1):
            acc = last_product(h)
            if h in GVT:
                nc.scalar.activation(o_woven[h][:], acc[:].rearrange("p t n -> p n t"), ACT.Copy, scale=OUT_SCALE)
            store_f32(h, acc)

        for t in range(PACK - 1):
            make_z(1, t, 0, HALF)
        for h in (2, 3):
            make_z(1, PACK - 1, h % 2 * CHUNK, CHUNK)
            nc.vector.tensor_copy(*z_views(h))
            acc = last_product(h)
            if h in GVT:
                nc.scalar.activation(o_woven[h][:], acc[:].rearrange("p t n -> p n t"), ACT.Copy, scale=OUT_SCALE)
            store_f32(h, acc)
        for h in range(PACK):
            if h not in GVT:
                nc.vector.tensor_copy(*weave_views(o_woven[h][:], o_f32[h][:]))
            make_planes(h)
        for q in range(4):
            queue = (nc.sync, nc.scalar)[q % 2]
            queue.dma_start(out_2[0, 4 * q : 4 * q + 4, :].bitcast(I32), o_s[32 * q : 32 * q + 4, :].bitcast(I32))
